import numpy as np
import ml_dtypes

BF16 = ml_dtypes.bfloat16


def bf(x):
    return np.asarray(x, np.float32).astype(BF16)


def f32(x):
    return np.asarray(x, np.float32)


def f64(x):
    return np.asarray(x).astype(np.float64)


def striped(idx):
    return np.tile(idx.reshape(-1, 16).T, (8, 1))


S, K, M, N, E, Q, O = 512, 128, 384, 128, 1, 128, 128


def sigmoid(v):
    return 1.0 / (1.0 + np.exp(-v))


def setup_inputs():
    return {"base": bf(np.random.standard_normal((M, S))), "x": bf(np.random.standard_normal((K, N))), "w": bf(1.2 * np.random.standard_normal((E, K, M)) / np.sqrt(K)), "w2": bf(np.random.standard_normal((M, O)) / np.sqrt(2 * M)), "b": f32(0.5 * np.random.standard_normal((O, 1))), "offs": striped(np.random.permutation(S)[:N])}


def reference(base, x, w, w2, b, offs):
    idx = offs[:16].T.reshape(-1)
    z = f64(base).copy()
    for e in range(E):
        z[:, idx[e * Q : (e + 1) * Q]] += f64(w)[e].T @ f64(x)[:, e * Q : (e + 1) * Q]
    y = f64(w2).T @ z
    return (y + f64(b)) * sigmoid(y + f64(b))

@@ -1,0 +1,67 @@
+import concourse.mybir as mybir
+from concourse.masks import make_identity
+
+BF16, F32, U16 = mybir.dt.bfloat16, mybir.dt.float32, mybir.dt.uint16
+SILU = mybir.ActivationFunctionType.Silu
+P = 128
+
+FLOPS = 2 * 128 * 384 * 128 + 2 * 384 * 128 * 512
+
+
+def tile_rows_thenproj_silu_kernel(tc, base, x, w, w2, b, offs, out):
+    nc = tc.nc
+    M, S = base.shape
+    N = x.shape[1]
+    O = w2.shape[1]
+    blocks = M // P
+
+    with (
+        tc.tile_pool(name="held", bufs=1) as held,
+        tc.psum_pool(name="psum", bufs=1) as psum,
+    ):
+        offsets = held.tile([P, N // 16], U16, name="offsets")
+        base_rows = [held.tile([P, S], BF16, name=f"base{a}") for a in range(blocks)]
+        x_tile = held.tile([P, N], BF16, name="x_tile")
+        w_tile = held.tile([P, M], BF16, name="w_tile")
+        w2_tile = held.tile([P, blocks, O], BF16, name="w2_tile")
+        bias = held.tile([P, 1], F32, name="bias")
+
+        nc.sync.dma_start(base_rows[0][:], base[0:P, :])
+        nc.scalar.dma_start(w_tile[:], w.rearrange("e k m -> (e k) m"))
+        nc.sync.dma_start(base_rows[1][:], base[P:2 * P, :])
+        nc.scalar.dma_start(x_tile[:], x)
+        nc.sync.dma_start(base_rows[2][:], base[2 * P:3 * P, :])
+        nc.sync.dma_start(offsets[:], offs)
+        nc.scalar.dma_start(w2_tile[:], w2.rearrange("(a p) o -> p a o", p=P))
+        nc.scalar.dma_start(bias[:], b)
+
+        zero_column = held.tile([P, 1], F32, name="zero_column")
+        table_loaded = held.tile([P, 1], F32, name="table_loaded")
+        nc.vector.memset(zero_column[:], 0.0)
+        nc.scalar.activation(table_loaded[:], zero_column[:], SILU)
+
+        identity = held.tile([P, P], BF16, name="identity")
+        make_identity(nc, identity[:])
+
+        windows = [psum.tile([P, S], F32, name=f"window{a}") for a in range(blocks)]
+        for a in range(blocks):
+            nc.tensor.matmul(windows[a][:], identity[:], base_rows[a][:], start=True, stop=False)
+
+        for a in range(blocks):
+            nc.tensor.matmul(
+                windows[a][:].indirect(offsets[:]), w_tile[:, a * P:(a + 1) * P], x_tile[:], start=False, stop=True
+            )
+
+        z = [held.tile([P, S], BF16, name=f"z{a}") for a in range(blocks)]
+        for a in range(blocks):
+            if a % 2 == 0:
+                nc.vector.tensor_copy(z[a][:], windows[a][:])
+            else:
+                nc.scalar.copy(z[a][:], windows[a][:])
+
+        y = psum.tile([O, S], F32, name="y")
+        for a in range(blocks):
+            nc.tensor.matmul(y[:], w2_tile[:, a, :], z[a][:], start=a == 0, stop=a == blocks - 1)
+        result = held.tile([O, S], F32, name="result")
+        nc.scalar.activation(result[:], y[:], SILU, bias=bias[:])
+        nc.sync.dma_start(out, result[:])

@@ -4,6 +4,7 @@ from concourse.masks import make_identity
 BF16, F32, U16 = mybir.dt.bfloat16, mybir.dt.float32, mybir.dt.uint16
 SILU = mybir.ActivationFunctionType.Silu
 P = 128
+WARM_UPS = 4
 
 FLOPS = 2 * 128 * 384 * 128 + 2 * 384 * 128 * 512
 
@@ -39,6 +40,12 @@ def tile_rows_thenproj_silu_kernel(tc, base, x, w, w2, b, offs, out):
         table_loaded = held.tile([P, 1], F32, name="table_loaded")
         nc.vector.memset(zero_column[:], 0.0)
         nc.scalar.activation(table_loaded[:], zero_column[:], SILU)
+
+        zeros = held.tile([P, S], BF16, name="zeros")
+        nc.vector.memset(zeros[:], 0.0)
+        spare = psum.tile([P, S], F32, name="spare")
+        for warm_up in range(WARM_UPS):
+            nc.tensor.matmul(spare[:], zeros[:, :P], zeros[:], start=True, stop=True)
 
         identity = held.tile([P, P], BF16, name="identity")
         make_identity(nc, identity[:])

@@ -4,7 +4,7 @@ from concourse.masks import make_identity
 BF16, F32, U16 = mybir.dt.bfloat16, mybir.dt.float32, mybir.dt.uint16
 SILU = mybir.ActivationFunctionType.Silu
 P = 128
-WARM_UPS = 4
+WARM_UPS = 3
 
 FLOPS = 2 * 128 * 384 * 128 + 2 * 384 * 128 * 512
 
@@ -27,22 +27,22 @@ def tile_rows_thenproj_silu_kernel(tc, base, x, w, w2, b, offs, out):
         w2_tile = held.tile([P, blocks, O], BF16, name="w2_tile")
         bias = held.tile([P, 1], F32, name="bias")
 
-        nc.sync.dma_start(base_rows[0][:], base[0:P, :])
-        nc.scalar.dma_start(w_tile[:], w.rearrange("e k m -> (e k) m"))
-        nc.sync.dma_start(base_rows[1][:], base[P:2 * P, :])
-        nc.scalar.dma_start(x_tile[:], x)
-        nc.sync.dma_start(base_rows[2][:], base[2 * P:3 * P, :])
+        for a in range(blocks):
+            nc.sync.dma_start(base_rows[a][:], base[a * P:(a + 1) * P, :])
         nc.sync.dma_start(offsets[:], offs)
-        nc.scalar.dma_start(w2_tile[:], w2.rearrange("(a p) o -> p a o", p=P))
-        nc.scalar.dma_start(bias[:], b)
+        nc.scalar.dma_start(w_tile[:], w.rearrange("e k m -> (e k) m"))
+        nc.scalar.dma_start(x_tile[:], x)
+        nc.sync.dma_start(w2_tile[:], w2.rearrange("(a p) o -> p a o", p=P))
+        nc.sync.dma_start(bias[:], b)
+
+        zeros = held.tile([P, S], BF16, name="zeros")
+        nc.vector.memset(zeros[:], 0.0)
 
         zero_column = held.tile([P, 1], F32, name="zero_column")
         table_loaded = held.tile([P, 1], F32, name="table_loaded")
         nc.vector.memset(zero_column[:], 0.0)
         nc.scalar.activation(table_loaded[:], zero_column[:], SILU)
 
-        zeros = held.tile([P, S], BF16, name="zeros")
-        nc.vector.memset(zeros[:], 0.0)
         spare = psum.tile([P, S], F32, name="spare")
         for warm_up in range(WARM_UPS):
             nc.tensor.matmul(spare[:], zeros[:, :P], zeros[:], start=True, stop=True)
@@ -59,16 +59,19 @@ def tile_rows_thenproj_silu_kernel(tc, base, x, w, w2, b, offs, out):
                 windows[a][:].indirect(offsets[:]), w_tile[:, a * P:(a + 1) * P], x_tile[:], start=False, stop=True
             )
 
+        halves = [slice(h * S // 2, (h + 1) * S // 2) for h in range(2)]
         z = [held.tile([P, S], BF16, name=f"z{a}") for a in range(blocks)]
         for a in range(blocks):
-            if a % 2 == 0:
-                nc.vector.tensor_copy(z[a][:], windows[a][:])
-            else:
-                nc.scalar.copy(z[a][:], windows[a][:])
+            for half in halves:
+                if a % 2 == 0:
+                    nc.vector.tensor_copy(z[a][:, half], windows[a][:, half])
+                else:
+                    nc.scalar.copy(z[a][:, half], windows[a][:, half])
 
-        y = psum.tile([O, S], F32, name="y")
-        for a in range(blocks):
-            nc.tensor.matmul(y[:], w2_tile[:, a, :], z[a][:], start=a == 0, stop=a == blocks - 1)
-        result = held.tile([O, S], F32, name="result")
-        nc.scalar.activation(result[:], y[:], SILU, bias=bias[:])
-        nc.sync.dma_start(out, result[:])
+        for h, half in enumerate(halves):
+            y = psum.tile([O, S // 2], F32, name=f"y{h}")
+            for a in range(blocks):
+                nc.tensor.matmul(y[:], w2_tile[:, a, :], z[a][:, half], start=a == 0, stop=a == blocks - 1)
+            result = held.tile([O, S // 2], F32, name=f"result{h}")
+            nc.scalar.activation(result[:], y[:], SILU, bias=bias[:])
+            nc.sync.dma_start(out[:, half], result[:])

@@ -29,9 +29,9 @@ def tile_rows_thenproj_silu_kernel(tc, base, x, w, w2, b, offs, out):
 
         for a in range(blocks):
             nc.sync.dma_start(base_rows[a][:], base[a * P:(a + 1) * P, :])
+        nc.sync.dma_start(w_tile[:], w.rearrange("e k m -> (e k) m"))
+        nc.sync.dma_start(x_tile[:], x)
         nc.sync.dma_start(offsets[:], offs)
-        nc.scalar.dma_start(w_tile[:], w.rearrange("e k m -> (e k) m"))
-        nc.scalar.dma_start(x_tile[:], x)
         nc.sync.dma_start(w2_tile[:], w2.rearrange("(a p) o -> p a o", p=P))
         nc.sync.dma_start(bias[:], b)
 

@@ -4,6 +4,7 @@ from concourse.masks import make_identity
 BF16, F32, U16 = mybir.dt.bfloat16, mybir.dt.float32, mybir.dt.uint16
 SILU = mybir.ActivationFunctionType.Silu
 P = 128
+PIECES = 4
 WARM_UPS = 3
 
 FLOPS = 2 * 128 * 384 * 128 + 2 * 384 * 128 * 512
@@ -59,19 +60,20 @@ def tile_rows_thenproj_silu_kernel(tc, base, x, w, w2, b, offs, out):
                 windows[a][:].indirect(offsets[:]), w_tile[:, a * P:(a + 1) * P], x_tile[:], start=False, stop=True
             )
 
-        halves = [slice(h * S // 2, (h + 1) * S // 2) for h in range(2)]
         z = [held.tile([P, S], BF16, name=f"z{a}") for a in range(blocks)]
-        for a in range(blocks):
-            for half in halves:
-                if a % 2 == 0:
-                    nc.vector.tensor_copy(z[a][:, half], windows[a][:, half])
-                else:
-                    nc.scalar.copy(z[a][:, half], windows[a][:, half])
-
-        for h, half in enumerate(halves):
-            y = psum.tile([O, S // 2], F32, name=f"y{h}")
+        width = S // PIECES
+        pieces = [slice(i * width, (i + 1) * width) for i in range(PIECES)]
+        for piece in pieces:
             for a in range(blocks):
-                nc.tensor.matmul(y[:], w2_tile[:, a, :], z[a][:, half], start=a == 0, stop=a == blocks - 1)
-            result = held.tile([O, S // 2], F32, name=f"result{h}")
+                if a % 2 == 0:
+                    nc.vector.tensor_copy(z[a][:, piece], windows[a][:, piece])
+                else:
+                    nc.scalar.copy(z[a][:, piece], windows[a][:, piece])
+
+        for i, piece in enumerate(pieces):
+            y = psum.tile([O, width], F32, name=f"y{i}")
+            for a in range(blocks):
+                nc.tensor.matmul(y[:], w2_tile[:, a, :], z[a][:, piece], start=a == 0, stop=a == blocks - 1)
+            result = held.tile([O, width], F32, name=f"result{i}")
             nc.scalar.activation(result[:], y[:], SILU, bias=bias[:])
-            nc.sync.dma_start(out[:, half], result[:])
+            nc.sync.dma_start(out[:, piece], result[:])

import concourse.mybir as mybir
from concourse.masks import make_identity

BF16, F32, U16 = mybir.dt.bfloat16, mybir.dt.float32, mybir.dt.uint16
SILU = mybir.ActivationFunctionType.Silu
P = 128
PIECES = 4
WARM_UPS = 3

FLOPS = 2 * 128 * 384 * 128 + 2 * 384 * 128 * 512


def tile_rows_thenproj_silu_kernel(tc, base, x, w, w2, b, offs, out):
    nc = tc.nc
    M, S = base.shape
    N = x.shape[1]
    O = w2.shape[1]
    blocks = M // P

    with (
        tc.tile_pool(name="held", bufs=1) as held,
        tc.psum_pool(name="psum", bufs=1) as psum,
    ):
        offsets = held.tile([P, N // 16], U16, name="offsets")
        base_rows = [held.tile([P, S], BF16, name=f"base{a}") for a in range(blocks)]
        x_tile = held.tile([P, N], BF16, name="x_tile")
        w_tile = held.tile([P, M], BF16, name="w_tile")
        w2_tile = held.tile([P, blocks, O], BF16, name="w2_tile")
        bias = held.tile([P, 1], F32, name="bias")

        for a in range(blocks):
            nc.sync.dma_start(base_rows[a][:], base[a * P:(a + 1) * P, :])
        nc.sync.dma_start(w_tile[:], w.rearrange("e k m -> (e k) m"))
        nc.sync.dma_start(x_tile[:], x)
        nc.sync.dma_start(offsets[:], offs)
        nc.sync.dma_start(w2_tile[:], w2.rearrange("(a p) o -> p a o", p=P))
        nc.sync.dma_start(bias[:], b)

        zeros = held.tile([P, S], BF16, name="zeros")
        nc.vector.memset(zeros[:], 0.0)

        zero_column = held.tile([P, 1], F32, name="zero_column")
        table_loaded = held.tile([P, 1], F32, name="table_loaded")
        nc.vector.memset(zero_column[:], 0.0)
        nc.scalar.activation(table_loaded[:], zero_column[:], SILU)

        spare = psum.tile([P, S], F32, name="spare")
        for warm_up in range(WARM_UPS):
            nc.tensor.matmul(spare[:], zeros[:, :P], zeros[:], start=True, stop=True)

        identity = held.tile([P, P], BF16, name="identity")
        make_identity(nc, identity[:])

        windows = [psum.tile([P, S], F32, name=f"window{a}") for a in range(blocks)]
        for a in range(blocks):
            nc.tensor.matmul(windows[a][:], identity[:], base_rows[a][:], start=True, stop=False)

        for a in range(blocks):
            nc.tensor.matmul(
                windows[a][:].indirect(offsets[:]), w_tile[:, a * P:(a + 1) * P], x_tile[:], start=False, stop=True
            )

        z = [held.tile([P, S], BF16, name=f"z{a}") for a in range(blocks)]
        width = S // PIECES
        pieces = [slice(i * width, (i + 1) * width) for i in range(PIECES)]
        for piece in pieces:
            for a in range(blocks):
                if a % 2 == 0:
                    nc.vector.tensor_copy(z[a][:, piece], windows[a][:, piece])
                else:
                    nc.scalar.copy(z[a][:, piece], windows[a][:, piece])

        for i, piece in enumerate(pieces):
            y = psum.tile([O, width], F32, name=f"y{i}")
            for a in range(blocks):
                nc.tensor.matmul(y[:], w2_tile[:, a, :], z[a][:, piece], start=a == 0, stop=a == blocks - 1)
            result = held.tile([O, width], F32, name=f"result{i}")
            nc.scalar.activation(result[:], y[:], SILU, bias=bias[:])
            nc.sync.dma_start(out[:, piece], result[:])
